import numpy as np
import ml_dtypes


def mxq(x, axis, fmt="e4m3"):
    dtype, down = {"e4m3": (ml_dtypes.float8_e4m3fn, 7), "e5m2": (ml_dtypes.float8_e5m2, 14)}[fmt]
    v = np.moveaxis(np.asarray(x, np.float32).astype(ml_dtypes.bfloat16).astype(np.float64), axis, -1)
    blocks = v.reshape(v.shape[:-1] + (-1, 32))
    amax = np.abs(blocks).max(-1, keepdims=True)
    byte = np.maximum(np.where(amax > 0, np.frexp(amax)[1] - 1 + 127, 0) - down, 1)
    scale = np.exp2(byte - 127.0)
    codes = (blocks / scale).astype(np.float32).astype(dtype).astype(np.float64)
    return np.moveaxis((codes * scale).reshape(v.shape), -1, axis)


WIDE = False


def mx_kscale(k):
    if not WIDE:
        return np.ones(k)
    levels = np.array([10, -10, 5, -5, 0])
    if k % 512:
        return np.exp2(np.random.permutation(np.resize(levels, k // 32))).repeat(32)
    a = np.empty((k // 512, 16))
    for p in range(k // 512):
        a[p, :8] = np.random.permutation(np.resize(levels, 8))
        for g in range(8):
            far = levels[np.abs(levels - a[p, g]) >= 10]
            a[p, g + 8] = far[np.random.randint(len(far))]
    return np.exp2(a.ravel()).repeat(32)


def f64(x):
    return np.asarray(x).astype(np.float64)


def striped(idx):
    return np.tile(idx.reshape(-1, 16).T, (8, 1)).astype(np.uint16)


def unstriped(offs):
    return offs[:16].T.reshape(-1).astype(np.int64)


def silu(v):
    return v / (1.0 + np.exp(-np.maximum(v, -700.0)))


K, T, E, C, N = 512, 1024, 16, 128, 128


def by_expert(wq, xq):
    return np.concatenate([wq[e].T @ xq[:, e * C:(e + 1) * C] for e in range(E)], axis=1)


def setup_inputs():
    n = np.random.standard_normal
    s = mx_kscale(K)[:, None]
    first = np.random.permutation(np.repeat(np.arange(E), T // E))
    second = (first + 1 + np.random.permutation(np.repeat(np.arange(E - 1), -(-T // (E - 1)))[:T])) % E
    while np.bincount(second, minlength=E).max() != T // E:
        load = np.bincount(second, minlength=E); hi, lo = int(load.argmax()), int(load.argmin())
        t = np.flatnonzero((second == hi) & (first != lo))[0]; second[t] = lo
    slot_token = np.empty(E * C, np.int64); pos = np.empty((2, T), np.int64); fill = np.zeros(E, np.int64)
    place = np.stack([np.random.permutation(C) for _ in range(E)])
    for r, deal in enumerate((first, second)):
        for t in np.random.permutation(T):
            e = deal[t]; j = e * C + place[e, fill[e]]; fill[e] += 1; slot_token[j] = t; pos[r, t] = j
    g = np.random.uniform(0.2, 0.8, T)
    return {
        "xT": (n((K, T)) * s).astype(np.float32),
        "w": (n((E, K, N)) / np.sqrt(K) / s[None]).astype(np.float32),
        "b": (0.3 * n((N, E))).astype(np.float32),
        "gate": np.stack([np.tile(g, (N, 1)), np.tile(1.0 - g, (N, 1))]).astype(np.float32),
        "offs": striped(slot_token),
        "pos1": striped(pos[0]),
        "pos2": striped(pos[1]),
    }


def reference(xT, w, b, gate, offs, pos1, pos2):
    idx = unstriped(offs)
    xq = mxq(f64(xT)[:, idx], 0, "e4m3")
    y = by_expert(mxq(f64(w), 1, "e4m3"), xq)
    y = silu(y + np.repeat(f64(b), C, axis=1))
    return f64(gate[0]) * y[:, unstriped(pos1)] + f64(gate[1]) * y[:, unstriped(pos2)]

@@ -1,0 +1,151 @@
+from contextlib import ExitStack
+
+import concourse.mybir as mybir
+
+K, T, E, C, N = 512, 1024, 16, 128, 128
+P = 128
+PACK = 4
+SLOTS = E * C
+
+FLOPS = 2 * K * N * SLOTS
+
+F32 = mybir.dt.float32
+BF16 = mybir.dt.bfloat16
+U32 = mybir.dt.uint32
+U16 = mybir.dt.uint16
+U8 = mybir.dt.uint8
+FP8X4 = mybir.dt.float8_e4m3fn_x4
+MULT = mybir.AluOpType.mult
+ADD = mybir.AluOpType.add
+SILU = mybir.ActivationFunctionType.Silu
+
+X_CHUNKS = (512, 256, 256)
+V_SHARE = 11 / 16
+W_CHUNK = 2
+GPSIMD_CHUNKS = (3, 5)
+SLOT_SLICES = (768, 768, 384, 128)
+TOKEN_PIECES = (512, 256, 256)
+
+
+def interleaved(bf):
+    return bf.rearrange("p (c i) t -> p c t i", i=4)
+
+
+def planes(raw):
+    return raw.rearrange("p t (c i) -> p c t i", i=4)
+
+
+def tile_routed_moe_kernel(tc, xT, w, b, gate, offs, pos1, pos2, out):
+    nc = tc.nc
+    with ExitStack() as ctx:
+        keep = ctx.enter_context(tc.tile_pool(name="keep", bufs=1))
+        psum = ctx.enter_context(tc.psum_pool(name="psum", bufs=8))
+
+        offs_sb = keep.tile([P, SLOTS // 16], U16, name="offs_sb")
+        pos1_sb = keep.tile([P, T // 16], U16, name="pos1_sb")
+        pos2_sb = keep.tile([P, T // 16], U16, name="pos2_sb")
+        b_sb = keep.tile([P, E], F32, name="b_sb")
+        warm = keep.tile([P, 1], F32, name="warm")
+        x_codes = keep.tile([P, T], U32, name="x_codes", align_bytes=64)
+        x_scales = keep.tile([P, T], U8, name="x_scales", align_bytes=64)
+        s_codes = keep.tile([P, SLOTS], U32, name="s_codes", align_bytes=64)
+        s_scales = keep.tile([P, SLOTS], U8, name="s_scales", align_bytes=64)
+        y_sb = keep.tile([P, SLOTS], F32, name="y_sb")
+        gate_sb = keep.tile([P, 2, T], F32, name="gate_sb")
+
+        nc.gpsimd.memset(x_scales[:], 0)
+        nc.vector.memset(warm[:], 0.0)
+        nc.scalar.activation(out=warm[:], in_=warm[:], func=SILU)
+
+        x_view = xT.rearrange("(p t) n -> p t n", t=PACK)
+        x_raw = []
+        t0 = 0
+        for i, width in enumerate(X_CHUNKS):
+            raw = keep.tile([P, PACK, width], F32, name=f"x_raw{i}")
+            nc.sync.dma_start(out=raw[:], in_=x_view[:, :, t0 : t0 + width])
+            x_raw.append(raw)
+            t0 += width
+        nc.sync.dma_start(offs_sb[:], offs)
+        w_view = w.rearrange("e (p t) n -> p e t n", t=PACK)
+        w_raw = []
+        for i in range(E // W_CHUNK):
+            raw = keep.tile([P, W_CHUNK, PACK, N], F32, name=f"w_raw{i}")
+            nc.sync.dma_start(out=raw[:], in_=w_view[:, i * W_CHUNK : (i + 1) * W_CHUNK])
+            w_raw.append(raw)
+            if i == 0:
+                nc.sync.dma_start(b_sb[:], b)
+        nc.sync.dma_start(pos1_sb[:], pos1)
+        nc.sync.dma_start(pos2_sb[:], pos2)
+        nc.sync.dma_start(out=gate_sb[:], in_=gate.rearrange("g p t -> p g t"))
+
+        t0 = 0
+        for i, width in enumerate(X_CHUNKS):
+            grouped = keep.tile([P, width, PACK], BF16, name=f"x_grouped{i}", align_bytes=64)
+            cut = int(width * V_SHARE)
+            nc.vector.tensor_copy(out=interleaved(grouped[:, :cut, :]), in_=planes(x_raw[i][:, :, :cut]))
+            nc.scalar.copy(out=interleaved(grouped[:, cut:, :]), in_=planes(x_raw[i][:, :, cut:]))
+            nc.vector.quantize_mx(
+                out=x_codes[:, t0 : t0 + width].bitcast(FP8X4),
+                scales=x_scales[:, t0 : t0 + width],
+                in_=grouped[:].rearrange("p c t -> p (c t)"),
+            )
+            t0 += width
+
+        w_codes, w_scales = [], []
+        for i in range(E // W_CHUNK):
+            grouped = keep.tile([P, W_CHUNK, N, PACK], BF16, name=f"w_grouped{i}", align_bytes=64)
+            codes = keep.tile([P, W_CHUNK * N], U32, name=f"w_codes{i}", align_bytes=64)
+            scales = keep.tile([P, W_CHUNK * N], U8, name=f"w_scales{i}", align_bytes=64)
+            dst = grouped[:].rearrange("p e (c i) t -> p e c t i", i=4)
+            src = w_raw[i][:].rearrange("p e t (c i) -> p e c t i", i=4)
+            if i in GPSIMD_CHUNKS:
+                for u in range(W_CHUNK):
+                    nc.gpsimd.tensor_scalar(
+                        out=interleaved(grouped[:, u]), in0=planes(w_raw[i][:, u]), scalar1=1.0, scalar2=0.0, op0=MULT, op1=ADD
+                    )
+            else:
+                nc.scalar.copy(out=dst, in_=src)
+            nc.vector.quantize_mx(
+                out=codes[:].bitcast(FP8X4),
+                scales=scales[:],
+                in_=grouped[:].rearrange("p e c t -> p (e c t)"),
+            )
+            w_codes.append(codes)
+            w_scales.append(scales)
+
+        j0 = 0
+        for width in SLOT_SLICES:
+            cols = slice(j0, j0 + width)
+            picks = offs_sb[:, j0 // 16 : (j0 + width) // 16]
+            nc.vector.tensor_copy(s_codes[:, cols], x_codes[:].indirect(picks))
+            nc.vector.tensor_copy(s_scales[:, cols], x_scales[:].indirect(picks))
+            for e in range(j0 // C, (j0 + width) // C):
+                slots = slice(e * C, (e + 1) * C)
+                w_cols = slice((e % W_CHUNK) * N, (e % W_CHUNK + 1) * N)
+                acc = psum.tile([N, C], F32, name="acc")
+                nc.tensor.matmul_mx(
+                    out=acc[:],
+                    lhsT=w_codes[e // W_CHUNK][:, w_cols].bitcast(FP8X4),
+                    lhsT_scale=w_scales[e // W_CHUNK][:, w_cols],
+                    rhs=s_codes[:, slots].bitcast(FP8X4),
+                    rhs_scale=s_scales[:, slots],
+                    start=True,
+                    stop=True,
+                )
+                nc.scalar.activation(out=y_sb[:, slots], in_=acc[:], func=SILU, bias=b_sb[:, e : e + 1])
+            j0 += width
+
+        t0 = 0
+        for i, width in enumerate(TOKEN_PIECES):
+            cols = slice(t0, t0 + width)
+            parts = []
+            for r, pos_sb in enumerate((pos1_sb, pos2_sb)):
+                part = keep.tile([P, width], F32, name=f"part{r}_{i}")
+                nc.vector.tensor_tensor(
+                    part[:], y_sb[:].indirect(pos_sb[:, t0 // 16 : (t0 + width) // 16]), gate_sb[:, r, cols], MULT
+                )
+                parts.append(part)
+            total = keep.tile([P, width], F32, name=f"total{i}")
+            nc.vector.tensor_add(out=total[:], in0=parts[0][:], in1=parts[1][:])
+            nc.sync.dma_start(out=out[:, cols], in_=total[:])
+            t0 += width

@@ -16,15 +16,13 @@ U16 = mybir.dt.uint16
 U8 = mybir.dt.uint8
 FP8X4 = mybir.dt.float8_e4m3fn_x4
 MULT = mybir.AluOpType.mult
-ADD = mybir.AluOpType.add
 SILU = mybir.ActivationFunctionType.Silu
 
 X_CHUNKS = (512, 256, 256)
 V_SHARE = 11 / 16
-W_CHUNK = 2
-GPSIMD_CHUNKS = (3, 5)
-SLOT_SLICES = (768, 768, 384, 128)
-TOKEN_PIECES = (512, 256, 256)
+W_GROUPS = ((0, 1, 2, 3), (4, 5, 6, 7), (12, 13, 10, 11), (8, 9), (14, 15))
+SLOT_SLICES = ((0, 768, "a", (768,)), (768, 768, "b", (768,)), (1536, 512, "b", (384, 128)))
+TOKEN_PIECES = (768, 256)
 
 
 def interleaved(bf):
@@ -39,6 +37,7 @@ def tile_routed_moe_kernel(tc, xT, w, b, gate, offs, pos1, pos2, out):
     nc = tc.nc
     with ExitStack() as ctx:
         keep = ctx.enter_context(tc.tile_pool(name="keep", bufs=1))
+        ring = ctx.enter_context(tc.tile_pool(name="ring", bufs=1))
         psum = ctx.enter_context(tc.psum_pool(name="psum", bufs=8))
 
         offs_sb = keep.tile([P, SLOTS // 16], U16, name="offs_sb")
@@ -48,8 +47,6 @@ def tile_routed_moe_kernel(tc, xT, w, b, gate, offs, pos1, pos2, out):
         warm = keep.tile([P, 1], F32, name="warm")
         x_codes = keep.tile([P, T], U32, name="x_codes", align_bytes=64)
         x_scales = keep.tile([P, T], U8, name="x_scales", align_bytes=64)
-        s_codes = keep.tile([P, SLOTS], U32, name="s_codes", align_bytes=64)
-        s_scales = keep.tile([P, SLOTS], U8, name="s_scales", align_bytes=64)
         y_sb = keep.tile([P, SLOTS], F32, name="y_sb")
         gate_sb = keep.tile([P, 2, T], F32, name="gate_sb")
 
@@ -67,13 +64,13 @@ def tile_routed_moe_kernel(tc, xT, w, b, gate, offs, pos1, pos2, out):
             t0 += width
         nc.sync.dma_start(offs_sb[:], offs)
         w_view = w.rearrange("e (p t) n -> p e t n", t=PACK)
-        w_raw = []
-        for i in range(E // W_CHUNK):
-            raw = keep.tile([P, W_CHUNK, PACK, N], F32, name=f"w_raw{i}")
-            nc.sync.dma_start(out=raw[:], in_=w_view[:, i * W_CHUNK : (i + 1) * W_CHUNK])
-            w_raw.append(raw)
-            if i == 0:
-                nc.sync.dma_start(b_sb[:], b)
+        w_raw = {}
+        for group in W_GROUPS:
+            for e in group[::2]:
+                raw = keep.tile([P, 2, PACK, N], F32, name=f"w_raw{e}")
+                nc.sync.dma_start(out=raw[:], in_=w_view[:, e : e + 2])
+                w_raw[e] = raw
+        nc.sync.dma_start(b_sb[:], b)
         nc.sync.dma_start(pos1_sb[:], pos1)
         nc.sync.dma_start(pos2_sb[:], pos2)
         nc.sync.dma_start(out=gate_sb[:], in_=gate.rearrange("g p t -> p g t"))
@@ -91,49 +88,76 @@ def tile_routed_moe_kernel(tc, xT, w, b, gate, offs, pos1, pos2, out):
             )
             t0 += width
 
-        w_codes, w_scales = [], []
-        for i in range(E // W_CHUNK):
-            grouped = keep.tile([P, W_CHUNK, N, PACK], BF16, name=f"w_grouped{i}", align_bytes=64)
-            codes = keep.tile([P, W_CHUNK * N], U32, name=f"w_codes{i}", align_bytes=64)
-            scales = keep.tile([P, W_CHUNK * N], U8, name=f"w_scales{i}", align_bytes=64)
-            dst = grouped[:].rearrange("p e (c i) t -> p e c t i", i=4)
-            src = w_raw[i][:].rearrange("p e t (c i) -> p e c t i", i=4)
-            if i in GPSIMD_CHUNKS:
-                for u in range(W_CHUNK):
-                    nc.gpsimd.tensor_scalar(
-                        out=interleaved(grouped[:, u]), in0=planes(w_raw[i][:, u]), scalar1=1.0, scalar2=0.0, op0=MULT, op1=ADD
-                    )
-            else:
-                nc.scalar.copy(out=dst, in_=src)
+        w_grouped = {}
+        for group in W_GROUPS:
+            grouped = keep.tile([P, len(group), N, PACK], BF16, name=f"w_grouped{group[0]}", align_bytes=64)
+            w_grouped[group] = grouped
+
+        def interleave_pair(group, e):
+            at = group.index(e)
+            nc.scalar.copy(
+                out=w_grouped[group][:, at : at + 2].rearrange("p e (c i) t -> p e c t i", i=4),
+                in_=w_raw[e][:].rearrange("p e t (c i) -> p e c t i", i=4),
+            )
+
+        def interleave_one(group, u, lo, hi):
+            nc.scalar.copy(
+                out=interleaved(w_grouped[group][:, u, lo:hi]), in_=planes(w_raw[group[0]][:, u, :, lo:hi])
+            )
+
+        w_codes, w_scales = {}, {}
+
+        def quantize(group):
+            codes = keep.tile([P, len(group) * N], U32, name=f"w_codes{group[0]}", align_bytes=64)
+            scales = keep.tile([P, len(group) * N], U8, name=f"w_scales{group[0]}", align_bytes=64)
             nc.vector.quantize_mx(
                 out=codes[:].bitcast(FP8X4),
                 scales=scales[:],
-                in_=grouped[:].rearrange("p e c t -> p (e c t)"),
+                in_=w_grouped[group][:].rearrange("p e c t -> p (e c t)"),
             )
-            w_codes.append(codes)
-            w_scales.append(scales)
+            for at, e in enumerate(group):
+                w_codes[e] = codes[:, at * N : (at + 1) * N]
+                w_scales[e] = scales[:, at * N : (at + 1) * N]
 
-        j0 = 0
-        for width in SLOT_SLICES:
-            cols = slice(j0, j0 + width)
-            picks = offs_sb[:, j0 // 16 : (j0 + width) // 16]
-            nc.vector.tensor_copy(s_codes[:, cols], x_codes[:].indirect(picks))
-            nc.vector.tensor_copy(s_scales[:, cols], x_scales[:].indirect(picks))
+        for group in W_GROUPS[:-2]:
+            for e in group[::2]:
+                interleave_pair(group, e)
+            quantize(group)
+        late, last = W_GROUPS[-2:]
+        interleave_one(late, 0, 0, N)
+        interleave_one(late, 1, 0, N // 2)
+        interleave_one(last, 0, 0, N)
+        interleave_one(late, 1, N // 2, N)
+        quantize(late)
+        interleave_one(last, 1, 0, N)
+        quantize(last)
+
+        for j0, width, tag, cuts in SLOT_SLICES:
+            s_codes = ring.tile([P, width], U32, name=f"s_codes_{tag}", align_bytes=64)
+            s_scales = ring.tile([P, width], U8, name=f"s_scales_{tag}", align_bytes=64)
+            nc.vector.tensor_copy(s_codes[:], x_codes[:].indirect(offs_sb[:, j0 // 16 : (j0 + width) // 16]))
+            c0 = 0
+            for cut in cuts:
+                nc.vector.tensor_copy(
+                    s_scales[:, c0 : c0 + cut],
+                    x_scales[:].indirect(offs_sb[:, (j0 + c0) // 16 : (j0 + c0 + cut) // 16]),
+                )
+                c0 += cut
             for e in range(j0 // C, (j0 + width) // C):
                 slots = slice(e * C, (e + 1) * C)
-                w_cols = slice((e % W_CHUNK) * N, (e % W_CHUNK + 1) * N)
-                acc = psum.tile([N, C], F32, name="acc")
+                own = slice(e * C - j0, (e + 1) * C - j0)
+                if e % 2 == 0:
+                    acc = psum.tile([N, 2, C], F32, name="acc")
                 nc.tensor.matmul_mx(
-                    out=acc[:],
-                    lhsT=w_codes[e // W_CHUNK][:, w_cols].bitcast(FP8X4),
-                    lhsT_scale=w_scales[e // W_CHUNK][:, w_cols],
-                    rhs=s_codes[:, slots].bitcast(FP8X4),
-                    rhs_scale=s_scales[:, slots],
+                    out=acc[:, e % 2],
+                    lhsT=w_codes[e].bitcast(FP8X4),
+                    lhsT_scale=w_scales[e],
+                    rhs=s_codes[:, own].bitcast(FP8X4),
+                    rhs_scale=s_scales[:, own],
                     start=True,
                     stop=True,
                 )
-                nc.scalar.activation(out=y_sb[:, slots], in_=acc[:], func=SILU, bias=b_sb[:, e : e + 1])
-            j0 += width
+                nc.scalar.activation(out=y_sb[:, slots], in_=acc[:, e % 2], func=SILU, bias=b_sb[:, e : e + 1])
 
         t0 = 0
         for i, width in enumerate(TOKEN_PIECES):

@@ -16,13 +16,16 @@ U16 = mybir.dt.uint16
 U8 = mybir.dt.uint8
 FP8X4 = mybir.dt.float8_e4m3fn_x4
 MULT = mybir.AluOpType.mult
+ADD = mybir.AluOpType.add
 SILU = mybir.ActivationFunctionType.Silu
 
 X_CHUNKS = (512, 256, 256)
 V_SHARE = 11 / 16
-W_GROUPS = ((0, 1, 2, 3), (4, 5, 6, 7), (12, 13, 10, 11), (8, 9), (14, 15))
+W_GROUPS = ((0, 1, 2, 3), (4, 5, 6, 7), (12, 13, 8, 9), (10, 11), (14, 15))
 SLOT_SLICES = ((0, 768, "a", (768,)), (768, 768, "b", (768,)), (1536, 512, "b", (384, 128)))
+BANKS = ((0, 1), (2, 3), (4, 5), (6, 7), (8, 9), (10, 11), (12, 13), (14,), (15,))
 TOKEN_PIECES = (768, 256)
+GPSIMD_PAIRS = (4, 12)
 
 
 def interleaved(bf):
@@ -43,7 +46,7 @@ def tile_routed_moe_kernel(tc, xT, w, b, gate, offs, pos1, pos2, out):
         offs_sb = keep.tile([P, SLOTS // 16], U16, name="offs_sb")
         pos1_sb = keep.tile([P, T // 16], U16, name="pos1_sb")
         pos2_sb = keep.tile([P, T // 16], U16, name="pos2_sb")
-        b_sb = keep.tile([P, E], F32, name="b_sb")
+        b_early = keep.tile([P, E], F32, name="b_early")
         warm = keep.tile([P, 1], F32, name="warm")
         x_codes = keep.tile([P, T], U32, name="x_codes", align_bytes=64)
         x_scales = keep.tile([P, T], U8, name="x_scales", align_bytes=64)
@@ -67,10 +70,13 @@ def tile_routed_moe_kernel(tc, xT, w, b, gate, offs, pos1, pos2, out):
         w_raw = {}
         for group in W_GROUPS:
             for e in group[::2]:
-                raw = keep.tile([P, 2, PACK, N], F32, name=f"w_raw{e}")
+                if group == W_GROUPS[-1]:
+                    raw = ring.tile([P, 2, PACK, N], F32, name="late")
+                else:
+                    raw = keep.tile([P, 2, PACK, N], F32, name=f"w_raw{e}")
                 nc.sync.dma_start(out=raw[:], in_=w_view[:, e : e + 2])
                 w_raw[e] = raw
-        nc.sync.dma_start(b_sb[:], b)
+        nc.sync.dma_start(b_early[:], b)
         nc.sync.dma_start(pos1_sb[:], pos1)
         nc.sync.dma_start(pos2_sb[:], pos2)
         nc.sync.dma_start(out=gate_sb[:], in_=gate.rearrange("g p t -> p g t"))
@@ -100,10 +106,16 @@ def tile_routed_moe_kernel(tc, xT, w, b, gate, offs, pos1, pos2, out):
                 in_=w_raw[e][:].rearrange("p e t (c i) -> p e c t i", i=4),
             )
 
-        def interleave_one(group, u, lo, hi):
-            nc.scalar.copy(
-                out=interleaved(w_grouped[group][:, u, lo:hi]), in_=planes(w_raw[group[0]][:, u, :, lo:hi])
-            )
+        def interleave_on_gpsimd(group, e):
+            for u in range(2):
+                nc.gpsimd.tensor_scalar(
+                    out=interleaved(w_grouped[group][:, group.index(e) + u]),
+                    in0=planes(w_raw[e][:, u]),
+                    scalar1=1.0,
+                    scalar2=0.0,
+                    op0=MULT,
+                    op1=ADD,
+                )
 
         w_codes, w_scales = {}, {}
 
@@ -119,18 +131,15 @@ def tile_routed_moe_kernel(tc, xT, w, b, gate, offs, pos1, pos2, out):
                 w_codes[e] = codes[:, at * N : (at + 1) * N]
                 w_scales[e] = scales[:, at * N : (at + 1) * N]
 
-        for group in W_GROUPS[:-2]:
+        for group in W_GROUPS:
             for e in group[::2]:
-                interleave_pair(group, e)
+                if e in GPSIMD_PAIRS:
+                    interleave_on_gpsimd(group, e)
+                else:
+                    interleave_pair(group, e)
             quantize(group)
-        late, last = W_GROUPS[-2:]
-        interleave_one(late, 0, 0, N)
-        interleave_one(late, 1, 0, N // 2)
-        interleave_one(last, 0, 0, N)
-        interleave_one(late, 1, N // 2, N)
-        quantize(late)
-        interleave_one(last, 1, 0, N)
-        quantize(last)
+        b_sb = ring.tile([P, E], F32, name="late")
+        nc.scalar.copy(out=b_sb[:], in_=b_early[:])
 
         for j0, width, tag, cuts in SLOT_SLICES:
             s_codes = ring.tile([P, width], U32, name=f"s_codes_{tag}", align_bytes=64)
@@ -143,21 +152,25 @@ def tile_routed_moe_kernel(tc, xT, w, b, gate, offs, pos1, pos2, out):
                     x_scales[:].indirect(offs_sb[:, (j0 + c0) // 16 : (j0 + c0 + cut) // 16]),
                 )
                 c0 += cut
-            for e in range(j0 // C, (j0 + width) // C):
-                slots = slice(e * C, (e + 1) * C)
-                own = slice(e * C - j0, (e + 1) * C - j0)
-                if e % 2 == 0:
-                    acc = psum.tile([N, 2, C], F32, name="acc")
-                nc.tensor.matmul_mx(
-                    out=acc[:, e % 2],
-                    lhsT=w_codes[e].bitcast(FP8X4),
-                    lhsT_scale=w_scales[e],
-                    rhs=s_codes[:, own].bitcast(FP8X4),
-                    rhs_scale=s_scales[:, own],
-                    start=True,
-                    stop=True,
-                )
-                nc.scalar.activation(out=y_sb[:, slots], in_=acc[:, e % 2], func=SILU, bias=b_sb[:, e : e + 1])
+            for bank in BANKS:
+                if not j0 <= bank[0] * C < j0 + width:
+                    continue
+                acc = psum.tile([N, len(bank), C], F32, name="acc")
+                for i, e in enumerate(bank):
+                    own = slice(e * C - j0, (e + 1) * C - j0)
+                    nc.tensor.matmul_mx(
+                        out=acc[:, i],
+                        lhsT=w_codes[e].bitcast(FP8X4),
+                        lhsT_scale=w_scales[e],
+                        rhs=s_codes[:, own].bitcast(FP8X4),
+                        rhs_scale=s_scales[:, own],
+                        start=True,
+                        stop=True,
+                    )
+                for i, e in enumerate(bank):
+                    nc.scalar.activation(
+                        out=y_sb[:, e * C : (e + 1) * C], in_=acc[:, i], func=SILU, bias=b_sb[:, e : e + 1]
+                    )
 
         t0 = 0
         for i, width in enumerate(TOKEN_PIECES):

@@ -6,6 +6,7 @@ K, T, E, C, N = 512, 1024, 16, 128, 128
 P = 128
 PACK = 4
 SLOTS = E * C
+STRIPE = 16
 
 FLOPS = 2 * K * N * SLOTS
 
@@ -16,23 +17,21 @@ U16 = mybir.dt.uint16
 U8 = mybir.dt.uint8
 FP8X4 = mybir.dt.float8_e4m3fn_x4
 MULT = mybir.AluOpType.mult
-ADD = mybir.AluOpType.add
 SILU = mybir.ActivationFunctionType.Silu
 
 X_CHUNKS = (512, 256, 256)
-V_SHARE = 11 / 16
-W_GROUPS = ((0, 1, 2, 3), (4, 5, 6, 7), (12, 13, 8, 9), (10, 11), (14, 15))
-SLOT_SLICES = ((0, 768, "a", (768,)), (768, 768, "b", (768,)), (1536, 512, "b", (384, 128)))
+VECTOR_SHARE = 11 / 16
+W_GROUPS = ((0, 1, 2, 3), (4, 5, 6, 7), (8, 9, 10, 11), (12, 13), (14,), (15,))
+SLOT_SLICES = (768, 768, 512)
 BANKS = ((0, 1), (2, 3), (4, 5), (6, 7), (8, 9), (10, 11), (12, 13), (14,), (15,))
 TOKEN_PIECES = (768, 256)
-GPSIMD_PAIRS = (4, 12)
 
 
-def interleaved(bf):
-    return bf.rearrange("p (c i) t -> p c t i", i=4)
+def by_columns(grouped):
+    return grouped.rearrange("p (c i) t -> p c t i", i=4)
 
 
-def planes(raw):
+def by_planes(raw):
     return raw.rearrange("p t (c i) -> p c t i", i=4)
 
 
@@ -40,126 +39,95 @@ def tile_routed_moe_kernel(tc, xT, w, b, gate, offs, pos1, pos2, out):
     nc = tc.nc
     with ExitStack() as ctx:
         keep = ctx.enter_context(tc.tile_pool(name="keep", bufs=1))
-        ring = ctx.enter_context(tc.tile_pool(name="ring", bufs=1))
+        turns = ctx.enter_context(tc.tile_pool(name="turns", bufs=1))
         psum = ctx.enter_context(tc.psum_pool(name="psum", bufs=8))
 
-        offs_sb = keep.tile([P, SLOTS // 16], U16, name="offs_sb")
-        pos1_sb = keep.tile([P, T // 16], U16, name="pos1_sb")
-        pos2_sb = keep.tile([P, T // 16], U16, name="pos2_sb")
-        b_early = keep.tile([P, E], F32, name="b_early")
-        warm = keep.tile([P, 1], F32, name="warm")
+        offs_sb = keep.tile([P, SLOTS // STRIPE], U16, name="offs_sb")
+        pos_sb = [keep.tile([P, T // STRIPE], U16, name=f"pos{r}_sb") for r in range(2)]
+        b_landed = keep.tile([P, E], F32, name="b_landed")
+        gate_sb = keep.tile([P, 2, T], F32, name="gate_sb")
         x_codes = keep.tile([P, T], U32, name="x_codes", align_bytes=64)
         x_scales = keep.tile([P, T], U8, name="x_scales", align_bytes=64)
         y_sb = keep.tile([P, SLOTS], F32, name="y_sb")
-        gate_sb = keep.tile([P, 2, T], F32, name="gate_sb")
 
         nc.gpsimd.memset(x_scales[:], 0)
+        warm = keep.tile([P, 1], F32, name="warm")
         nc.vector.memset(warm[:], 0.0)
         nc.scalar.activation(out=warm[:], in_=warm[:], func=SILU)
 
         x_view = xT.rearrange("(p t) n -> p t n", t=PACK)
+        x_starts = [sum(X_CHUNKS[:i]) for i in range(len(X_CHUNKS))]
         x_raw = []
-        t0 = 0
-        for i, width in enumerate(X_CHUNKS):
+        for i, (t0, width) in enumerate(zip(x_starts, X_CHUNKS)):
             raw = keep.tile([P, PACK, width], F32, name=f"x_raw{i}")
             nc.sync.dma_start(out=raw[:], in_=x_view[:, :, t0 : t0 + width])
             x_raw.append(raw)
-            t0 += width
         nc.sync.dma_start(offs_sb[:], offs)
         w_view = w.rearrange("e (p t) n -> p e t n", t=PACK)
         w_raw = {}
-        for group in W_GROUPS:
-            for e in group[::2]:
-                if group == W_GROUPS[-1]:
-                    raw = ring.tile([P, 2, PACK, N], F32, name="late")
-                else:
-                    raw = keep.tile([P, 2, PACK, N], F32, name=f"w_raw{e}")
-                nc.sync.dma_start(out=raw[:], in_=w_view[:, e : e + 2])
-                w_raw[e] = raw
-        nc.sync.dma_start(b_early[:], b)
-        nc.sync.dma_start(pos1_sb[:], pos1)
-        nc.sync.dma_start(pos2_sb[:], pos2)
+        for e in range(0, E, 2):
+            pool = turns if e >= E - 4 else keep
+            raw = pool.tile([P, 2, PACK, N], F32, name=f"w_raw{e}", align_bytes=64)
+            nc.sync.dma_start(out=raw[:], in_=w_view[:, e : e + 2])
+            w_raw[e] = raw
+        nc.sync.dma_start(b_landed[:], b)
+        nc.sync.dma_start(pos_sb[0][:], pos1)
+        nc.sync.dma_start(pos_sb[1][:], pos2)
         nc.sync.dma_start(out=gate_sb[:], in_=gate.rearrange("g p t -> p g t"))
 
-        t0 = 0
-        for i, width in enumerate(X_CHUNKS):
+        for i, (t0, width) in enumerate(zip(x_starts, X_CHUNKS)):
             grouped = keep.tile([P, width, PACK], BF16, name=f"x_grouped{i}", align_bytes=64)
-            cut = int(width * V_SHARE)
-            nc.vector.tensor_copy(out=interleaved(grouped[:, :cut, :]), in_=planes(x_raw[i][:, :, :cut]))
-            nc.scalar.copy(out=interleaved(grouped[:, cut:, :]), in_=planes(x_raw[i][:, :, cut:]))
+            cut = int(width * VECTOR_SHARE)
+            nc.vector.tensor_copy(out=by_columns(grouped[:, :cut, :]), in_=by_planes(x_raw[i][:, :, :cut]))
+            nc.scalar.copy(out=by_columns(grouped[:, cut:, :]), in_=by_planes(x_raw[i][:, :, cut:]))
             nc.vector.quantize_mx(
                 out=x_codes[:, t0 : t0 + width].bitcast(FP8X4),
                 scales=x_scales[:, t0 : t0 + width],
                 in_=grouped[:].rearrange("p c t -> p (c t)"),
             )
-            t0 += width
-
-        w_grouped = {}
-        for group in W_GROUPS:
-            grouped = keep.tile([P, len(group), N, PACK], BF16, name=f"w_grouped{group[0]}", align_bytes=64)
-            w_grouped[group] = grouped
-
-        def interleave_pair(group, e):
-            at = group.index(e)
-            nc.scalar.copy(
-                out=w_grouped[group][:, at : at + 2].rearrange("p e (c i) t -> p e c t i", i=4),
-                in_=w_raw[e][:].rearrange("p e t (c i) -> p e c t i", i=4),
-            )
-
-        def interleave_on_gpsimd(group, e):
-            for u in range(2):
-                nc.gpsimd.tensor_scalar(
-                    out=interleaved(w_grouped[group][:, group.index(e) + u]),
-                    in0=planes(w_raw[e][:, u]),
-                    scalar1=1.0,
-                    scalar2=0.0,
-                    op0=MULT,
-                    op1=ADD,
-                )
 
         w_codes, w_scales = {}, {}
-
-        def quantize(group):
+        for group in W_GROUPS:
+            grouped = keep.tile([P, len(group), N, PACK], BF16, name=f"w_grouped{group[0]}", align_bytes=64)
+            if len(group) == 1:
+                pair, one = group[0] - group[0] % 2, group[0] % 2
+                nc.scalar.copy(out=by_columns(grouped[:, 0]), in_=by_planes(w_raw[pair][:, one]))
+            else:
+                for at in range(0, len(group), 2):
+                    nc.scalar.copy(
+                        out=grouped[:, at : at + 2].rearrange("p e (c i) t -> p e c t i", i=4),
+                        in_=w_raw[group[at]][:].rearrange("p e t (c i) -> p e c t i", i=4),
+                    )
             codes = keep.tile([P, len(group) * N], U32, name=f"w_codes{group[0]}", align_bytes=64)
             scales = keep.tile([P, len(group) * N], U8, name=f"w_scales{group[0]}", align_bytes=64)
             nc.vector.quantize_mx(
-                out=codes[:].bitcast(FP8X4),
-                scales=scales[:],
-                in_=w_grouped[group][:].rearrange("p e c t -> p (e c t)"),
+                out=codes[:].bitcast(FP8X4), scales=scales[:], in_=grouped[:].rearrange("p e c t -> p (e c t)")
             )
             for at, e in enumerate(group):
                 w_codes[e] = codes[:, at * N : (at + 1) * N]
                 w_scales[e] = scales[:, at * N : (at + 1) * N]
 
-        for group in W_GROUPS:
-            for e in group[::2]:
-                if e in GPSIMD_PAIRS:
-                    interleave_on_gpsimd(group, e)
-                else:
-                    interleave_pair(group, e)
-            quantize(group)
-        b_sb = ring.tile([P, E], F32, name="late")
-        nc.scalar.copy(out=b_sb[:], in_=b_early[:])
+        b_sb = turns.tile([P, E], F32, name=f"w_raw{E - 2}", align_bytes=64)
+        nc.scalar.copy(out=b_sb[:], in_=b_landed[:])
 
-        for j0, width, tag, cuts in SLOT_SLICES:
-            s_codes = ring.tile([P, width], U32, name=f"s_codes_{tag}", align_bytes=64)
-            s_scales = ring.tile([P, width], U8, name=f"s_scales_{tag}", align_bytes=64)
-            nc.vector.tensor_copy(s_codes[:], x_codes[:].indirect(offs_sb[:, j0 // 16 : (j0 + width) // 16]))
-            c0 = 0
-            for cut in cuts:
-                nc.vector.tensor_copy(
-                    s_scales[:, c0 : c0 + cut],
-                    x_scales[:].indirect(offs_sb[:, (j0 + c0) // 16 : (j0 + c0 + cut) // 16]),
-                )
-                c0 += cut
+        j0 = 0
+        for i, width in enumerate(SLOT_SLICES):
+            if i == len(SLOT_SLICES) - 1:
+                s_codes = turns.tile([P, width], U32, name=f"w_raw{E - 4}", align_bytes=64)
+            else:
+                s_codes = keep.tile([P, width], U32, name=f"s_codes{i}", align_bytes=64)
+            s_scales = keep.tile([P, width], U8, name=f"s_scales{i}", align_bytes=64)
+            picks = offs_sb[:, j0 // STRIPE : (j0 + width) // STRIPE]
+            nc.vector.tensor_copy(s_codes[:], x_codes[:].indirect(picks))
+            nc.vector.tensor_copy(s_scales[:], x_scales[:].indirect(picks))
             for bank in BANKS:
                 if not j0 <= bank[0] * C < j0 + width:
                     continue
                 acc = psum.tile([N, len(bank), C], F32, name="acc")
-                for i, e in enumerate(bank):
+                for at, e in enumerate(bank):
                     own = slice(e * C - j0, (e + 1) * C - j0)
                     nc.tensor.matmul_mx(
-                        out=acc[:, i],
+                        out=acc[:, at],
                         lhsT=w_codes[e].bitcast(FP8X4),
                         lhsT_scale=w_scales[e],
                         rhs=s_codes[:, own].bitcast(FP8X4),
@@ -167,22 +135,31 @@ def tile_routed_moe_kernel(tc, xT, w, b, gate, offs, pos1, pos2, out):
                         start=True,
                         stop=True,
                     )
-                for i, e in enumerate(bank):
-                    nc.scalar.activation(
-                        out=y_sb[:, e * C : (e + 1) * C], in_=acc[:, i], func=SILU, bias=b_sb[:, e : e + 1]
-                    )
+                for at, e in enumerate(bank):
+                    slots = slice(e * C, (e + 1) * C)
+                    nc.scalar.activation(out=y_sb[:, slots], in_=acc[:, at], func=SILU, bias=b_sb[:, e : e + 1])
+            j0 += width
 
-        t0 = 0
-        for i, width in enumerate(TOKEN_PIECES):
-            cols = slice(t0, t0 + width)
-            parts = []
-            for r, pos_sb in enumerate((pos1_sb, pos2_sb)):
-                part = keep.tile([P, width], F32, name=f"part{r}_{i}")
-                nc.vector.tensor_tensor(
-                    part[:], y_sb[:].indirect(pos_sb[:, t0 // 16 : (t0 + width) // 16]), gate_sb[:, r, cols], MULT
-                )
-                parts.append(part)
-            total = keep.tile([P, width], F32, name=f"total{i}")
-            nc.vector.tensor_add(out=total[:], in0=parts[0][:], in1=parts[1][:])
+        starts = [sum(TOKEN_PIECES[:i]) for i in range(len(TOKEN_PIECES))]
+        parts = {}
+
+        def pick(i, r):
+            cols = slice(starts[i], starts[i] + TOKEN_PIECES[i])
+            picks = pos_sb[r][:, cols.start // STRIPE : cols.stop // STRIPE]
+            part = keep.tile([P, TOKEN_PIECES[i]], F32, name=f"part{r}_{i}")
+            nc.vector.tensor_tensor(part[:], y_sb[:].indirect(picks), gate_sb[:, r, cols], MULT)
+            parts[i, r] = part
+
+        def finish(i):
+            cols = slice(starts[i], starts[i] + TOKEN_PIECES[i])
+            total = keep.tile([P, TOKEN_PIECES[i]], F32, name=f"total{i}")
+            nc.vector.tensor_add(out=total[:], in0=parts[i, 0][:], in1=parts[i, 1][:])
             nc.sync.dma_start(out=out[:, cols], in_=total[:])
-            t0 += width
+
+        pick(0, 0)
+        pick(0, 1)
+        for i in range(1, len(TOKEN_PIECES)):
+            pick(i, 0)
+            finish(i - 1)
+            pick(i, 1)
+        finish(len(TOKEN_PIECES) - 1)

from contextlib import ExitStack

import concourse.mybir as mybir

K, T, E, C, N = 512, 1024, 16, 128, 128
P = 128
PACK = 4
SLOTS = E * C
STRIPE = 16

FLOPS = 2 * K * N * SLOTS

F32 = mybir.dt.float32
BF16 = mybir.dt.bfloat16
U32 = mybir.dt.uint32
U16 = mybir.dt.uint16
U8 = mybir.dt.uint8
FP8X4 = mybir.dt.float8_e4m3fn_x4
MULT = mybir.AluOpType.mult
SILU = mybir.ActivationFunctionType.Silu

X_CHUNKS = (512, 256, 256)
VECTOR_SHARE = 11 / 16
W_GROUPS = ((0, 1, 2, 3), (4, 5, 6, 7), (8, 9, 10, 11), (12, 13), (14,), (15,))
SLOT_SLICES = (768, 768, 512)
BANKS = ((0, 1), (2, 3), (4, 5), (6, 7), (8, 9), (10, 11), (12, 13), (14,), (15,))
TOKEN_PIECES = (768, 256)


def by_columns(grouped):
    return grouped.rearrange("p (c i) t -> p c t i", i=4)


def by_planes(raw):
    return raw.rearrange("p t (c i) -> p c t i", i=4)


def tile_routed_moe_kernel(tc, xT, w, b, gate, offs, pos1, pos2, out):
    nc = tc.nc
    with ExitStack() as ctx:
        keep = ctx.enter_context(tc.tile_pool(name="keep", bufs=1))
        turns = ctx.enter_context(tc.tile_pool(name="turns", bufs=1))
        psum = ctx.enter_context(tc.psum_pool(name="psum", bufs=8))

        offs_sb = keep.tile([P, SLOTS // STRIPE], U16, name="offs_sb")
        pos_sb = [keep.tile([P, T // STRIPE], U16, name=f"pos{r}_sb") for r in range(2)]
        b_landed = keep.tile([P, E], F32, name="b_landed")
        gate_sb = keep.tile([P, 2, T], F32, name="gate_sb")
        x_codes = keep.tile([P, T], U32, name="x_codes", align_bytes=64)
        x_scales = keep.tile([P, T], U8, name="x_scales", align_bytes=64)
        y_sb = keep.tile([P, SLOTS], F32, name="y_sb")

        nc.gpsimd.memset(x_scales[:], 0)
        warm = keep.tile([P, 1], F32, name="warm")
        nc.vector.memset(warm[:], 0.0)
        nc.scalar.activation(out=warm[:], in_=warm[:], func=SILU)

        x_view = xT.rearrange("(p t) n -> p t n", t=PACK)
        x_starts = [sum(X_CHUNKS[:i]) for i in range(len(X_CHUNKS))]
        x_raw = []
        for i, (t0, width) in enumerate(zip(x_starts, X_CHUNKS)):
            raw = keep.tile([P, PACK, width], F32, name=f"x_raw{i}")
            nc.sync.dma_start(out=raw[:], in_=x_view[:, :, t0 : t0 + width])
            x_raw.append(raw)
        nc.sync.dma_start(offs_sb[:], offs)
        w_view = w.rearrange("e (p t) n -> p e t n", t=PACK)
        w_raw = {}
        for e in range(0, E, 2):
            pool = turns if e >= E - 4 else keep
            raw = pool.tile([P, 2, PACK, N], F32, name=f"w_raw{e}", align_bytes=64)
            nc.sync.dma_start(out=raw[:], in_=w_view[:, e : e + 2])
            w_raw[e] = raw
        nc.sync.dma_start(b_landed[:], b)
        nc.sync.dma_start(pos_sb[0][:], pos1)
        nc.sync.dma_start(pos_sb[1][:], pos2)
        nc.sync.dma_start(out=gate_sb[:], in_=gate.rearrange("g p t -> p g t"))

        for i, (t0, width) in enumerate(zip(x_starts, X_CHUNKS)):
            grouped = keep.tile([P, width, PACK], BF16, name=f"x_grouped{i}", align_bytes=64)
            cut = int(width * VECTOR_SHARE)
            nc.vector.tensor_copy(out=by_columns(grouped[:, :cut, :]), in_=by_planes(x_raw[i][:, :, :cut]))
            nc.scalar.copy(out=by_columns(grouped[:, cut:, :]), in_=by_planes(x_raw[i][:, :, cut:]))
            nc.vector.quantize_mx(
                out=x_codes[:, t0 : t0 + width].bitcast(FP8X4),
                scales=x_scales[:, t0 : t0 + width],
                in_=grouped[:].rearrange("p c t -> p (c t)"),
            )

        w_codes, w_scales = {}, {}
        for group in W_GROUPS:
            grouped = keep.tile([P, len(group), N, PACK], BF16, name=f"w_grouped{group[0]}", align_bytes=64)
            if len(group) == 1:
                pair, one = group[0] - group[0] % 2, group[0] % 2
                nc.scalar.copy(out=by_columns(grouped[:, 0]), in_=by_planes(w_raw[pair][:, one]))
            else:
                for at in range(0, len(group), 2):
                    nc.scalar.copy(
                        out=grouped[:, at : at + 2].rearrange("p e (c i) t -> p e c t i", i=4),
                        in_=w_raw[group[at]][:].rearrange("p e t (c i) -> p e c t i", i=4),
                    )
            codes = keep.tile([P, len(group) * N], U32, name=f"w_codes{group[0]}", align_bytes=64)
            scales = keep.tile([P, len(group) * N], U8, name=f"w_scales{group[0]}", align_bytes=64)
            nc.vector.quantize_mx(
                out=codes[:].bitcast(FP8X4), scales=scales[:], in_=grouped[:].rearrange("p e c t -> p (e c t)")
            )
            for at, e in enumerate(group):
                w_codes[e] = codes[:, at * N : (at + 1) * N]
                w_scales[e] = scales[:, at * N : (at + 1) * N]

        b_sb = turns.tile([P, E], F32, name=f"w_raw{E - 2}", align_bytes=64)
        nc.scalar.copy(out=b_sb[:], in_=b_landed[:])

        j0 = 0
        for i, width in enumerate(SLOT_SLICES):
            if i == len(SLOT_SLICES) - 1:
                s_codes = turns.tile([P, width], U32, name=f"w_raw{E - 4}", align_bytes=64)
            else:
                s_codes = keep.tile([P, width], U32, name=f"s_codes{i}", align_bytes=64)
            s_scales = keep.tile([P, width], U8, name=f"s_scales{i}", align_bytes=64)
            picks = offs_sb[:, j0 // STRIPE : (j0 + width) // STRIPE]
            nc.vector.tensor_copy(s_codes[:], x_codes[:].indirect(picks))
            nc.vector.tensor_copy(s_scales[:], x_scales[:].indirect(picks))
            for bank in BANKS:
                if not j0 <= bank[0] * C < j0 + width:
                    continue
                acc = psum.tile([N, len(bank), C], F32, name="acc")
                for at, e in enumerate(bank):
                    own = slice(e * C - j0, (e + 1) * C - j0)
                    nc.tensor.matmul_mx(
                        out=acc[:, at],
                        lhsT=w_codes[e].bitcast(FP8X4),
                        lhsT_scale=w_scales[e],
                        rhs=s_codes[:, own].bitcast(FP8X4),
                        rhs_scale=s_scales[:, own],
                        start=True,
                        stop=True,
                    )
                for at, e in enumerate(bank):
                    slots = slice(e * C, (e + 1) * C)
                    nc.scalar.activation(out=y_sb[:, slots], in_=acc[:, at], func=SILU, bias=b_sb[:, e : e + 1])
            j0 += width

        starts = [sum(TOKEN_PIECES[:i]) for i in range(len(TOKEN_PIECES))]
        parts = {}

        def pick(i, r):
            cols = slice(starts[i], starts[i] + TOKEN_PIECES[i])
            picks = pos_sb[r][:, cols.start // STRIPE : cols.stop // STRIPE]
            part = keep.tile([P, TOKEN_PIECES[i]], F32, name=f"part{r}_{i}")
            nc.vector.tensor_tensor(part[:], y_sb[:].indirect(picks), gate_sb[:, r, cols], MULT)
            parts[i, r] = part

        def finish(i):
            cols = slice(starts[i], starts[i] + TOKEN_PIECES[i])
            total = keep.tile([P, TOKEN_PIECES[i]], F32, name=f"total{i}")
            nc.vector.tensor_add(out=total[:], in0=parts[i, 0][:], in1=parts[i, 1][:])
            nc.sync.dma_start(out=out[:, cols], in_=total[:])

        pick(0, 0)
        pick(0, 1)
        for i in range(1, len(TOKEN_PIECES)):
            pick(i, 0)
            finish(i - 1)
            pick(i, 1)
        finish(len(TOKEN_PIECES) - 1)
